import numpy as np
import ml_dtypes


def mxq(x, axis, fmt="e4m3"):
    dtype, down = {"e4m3": (ml_dtypes.float8_e4m3fn, 7), "e5m2": (ml_dtypes.float8_e5m2, 14)}[fmt]
    v = np.moveaxis(np.asarray(x, np.float32).astype(ml_dtypes.bfloat16).astype(np.float64), axis, -1)
    blocks = v.reshape(v.shape[:-1] + (-1, 32))
    amax = np.abs(blocks).max(-1, keepdims=True)
    byte = np.maximum(np.where(amax > 0, np.frexp(amax)[1] - 1 + 127, 0) - down, 1)
    scale = np.exp2(byte - 127.0)
    codes = (blocks / scale).astype(np.float32).astype(dtype).astype(np.float64)
    return np.moveaxis((codes * scale).reshape(v.shape), -1, axis)


WIDE = False


def mx_kscale(k):
    if not WIDE:
        return np.ones(k)
    levels = np.array([10, -10, 5, -5, 0])
    if k % 512:
        return np.exp2(np.random.permutation(np.resize(levels, k // 32))).repeat(32)
    a = np.empty((k // 512, 16))
    for p in range(k // 512):
        a[p, :8] = np.random.permutation(np.resize(levels, 8))
        for g in range(8):
            far = levels[np.abs(levels - a[p, g]) >= 10]
            a[p, g + 8] = far[np.random.randint(len(far))]
    return np.exp2(a.ravel()).repeat(32)


def f64(x):
    return np.asarray(x).astype(np.float64)


def striped(idx):
    return np.tile(idx.reshape(-1, 16).T, (8, 1)).astype(np.uint16)


def unstriped(offs):
    return offs[:16].T.reshape(-1).astype(np.int64)


E2M1 = np.array([0.0, 0.5, 1.0, 1.5, 2.0, 3.0, 4.0, 6.0, -0.0, -0.5, -1.0, -1.5, -2.0, -3.0, -4.0, -6.0])


def pack_weight(w, fmt):
    k, n = w.shape
    w = f64(np.asarray(w, np.float32).astype(ml_dtypes.bfloat16)).reshape(k // 32, 32, n)
    amax = np.abs(w).max(1)
    if fmt == "e4m3":
        byte = np.frexp(amax)[1] - 1 + 127 - 7
    else:
        mant, ex = np.frexp(amax / 6.0)
        byte = np.where(mant > 0.5, ex, ex - 1) + 127
    byte = np.clip(np.where(amax > 0, byte, 1), 1, 254)
    scaled = (w * np.exp2(127.0 - byte)[:, None, :]).reshape(k, n).astype(np.float32)
    by_word = np.ascontiguousarray(scaled.reshape(k // 512, 128, 4, n).transpose(0, 1, 3, 2))
    if fmt == "e4m3":
        words = by_word.astype(ml_dtypes.float8_e4m3fn).view(np.uint8)
    else:
        c = by_word.astype(ml_dtypes.float4_e2m1fn).view(np.uint8) & 0xF
        words = (c[..., 0::2] | (c[..., 1::2] << 4)).reshape(k // 512, 128, 2 * n)
    return np.ascontiguousarray(words), np.ascontiguousarray(byte.astype(np.uint8).reshape(k // 512, 16, n))


def unpack_weight(words, scales, fmt):
    g, _, n = scales.shape
    words = np.ascontiguousarray(words).reshape(g, 128, n, -1)
    if fmt == "e4m3":
        vals = words.view(ml_dtypes.float8_e4m3fn).astype(np.float64)
    else:
        nib = np.empty((g, 128, n, 4), np.uint8)
        nib[..., 0::2] = words & 0xF
        nib[..., 1::2] = words >> 4
        vals = E2M1[nib]
    vals = vals * np.repeat(np.exp2(scales.astype(np.float64) - 127.0), 8, axis=1)[..., None]
    return vals.transpose(0, 1, 3, 2).reshape(g * 512, n)


def gelu(v):
    return 0.5 * v * (1.0 + np.tanh(np.sqrt(2.0 / np.pi) * (v + 0.044715 * v**3)))


K, H, T, S, P = 1024, 1024, 4096, 1024, 512

def setup_inputs():
    n = np.random.standard_normal
    s = mx_kscale(K)[:, None]
    u = mx_kscale(H)[:, None]
    tab_words, tab_scales = pack_weight(n((K, T)) * s, "e4m3")
    w1 = n((K, H)) / np.sqrt(K) / s
    w2_words, w2_scales = pack_weight(1.5 * n((H, H)) / np.sqrt(H) / u, "e2m1")
    gain = np.exp(0.3 * n(H)) * u[:, 0]
    return {
        "tab_words": tab_words, "tab_scales": tab_scales,
        "offs": striped(np.random.permutation(T)[:S]),
        "w1": w1.astype(np.float32),
        "pos1": striped(np.random.permutation(S)[:P]),
        "pos2": striped(np.random.permutation(S)[:P]),
        "gain": gain.astype(np.float32),
        "w2_words": w2_words, "w2_scales": w2_scales,
    }

def reference(tab_words, tab_scales, offs, w1, pos1, pos2, gain, w2_words, w2_scales):
    v = unpack_weight(tab_words, tab_scales, "e4m3")[:, unstriped(offs)]
    w2 = unpack_weight(w2_words, w2_scales, "e2m1")
    h = mxq(f64(w1), 0, "e4m3").T @ v
    hp = h[:, unstriped(pos1)]
    x = 0.5 * hp * (1.0 + np.tanh(0.7978845608028654 * (hp + 0.044715 * hp * hp * hp)))
    x = x * f64(gain)[:, None]
    y = w2.T @ mxq(x, 0, "e4m3")
    hs = h[:, unstriped(pos2)]
    out = y * (1.0 / (1.0 + np.exp(-hs))) + hs
    return out

@@ -1,0 +1,277 @@
+from contextlib import ExitStack
+
+import concourse.mybir as mybir
+
+K, H, T, S, E = 1024, 1024, 4096, 1024, 512
+FLOPS = 2 * K * H * S + 2 * H * H * E
+
+F32 = mybir.dt.float32
+BF16 = mybir.dt.bfloat16
+I32 = mybir.dt.int32
+U32 = mybir.dt.uint32
+U16 = mybir.dt.uint16
+U8 = mybir.dt.uint8
+FP8X4 = mybir.dt.float8_e4m3fn_x4
+FP4X4 = mybir.dt.float4_e2m1fn_x4
+ALU = mybir.AluOpType
+ACT = mybir.ActivationFunctionType
+
+P = 128
+PACK = 4
+PASS = P * PACK
+BANK = 512
+
+
+def tile_list_larva_drift_step_kernel(
+    tc, tab_words, tab_scales, offs, w1, pos1, pos2, gain, w2_words, w2_scales, out
+):
+    nc = tc.nc
+    with ExitStack() as ctx:
+        lists = ctx.enter_context(tc.tile_pool(name="lists", bufs=1))
+        keep = ctx.enter_context(tc.tile_pool(name="keep", bufs=1))
+        psum = ctx.enter_context(tc.psum_pool(name="psum", bufs=1))
+
+        offs_sb = lists.tile([P, S // 16], U16, name="offs_sb")
+        pos1_sb = lists.tile([P, E // 16], U16, name="pos1_sb")
+        pos2_sb = lists.tile([P, E // 16], U16, name="pos2_sb")
+
+        def bank(i, name):
+            return psum.tile([P, BANK], F32, name=name, tag="bank%d" % i)
+
+        tab_sc = keep.tile([P, T], U8, name="tab_sc", align_bytes=64)
+        w2_sc_raw = keep.tile([P, H], U8, name="w2_sc_raw", align_bytes=64)
+        w2_sc = keep.tile([P, 2 * H], U8, name="w2_sc", align_bytes=64)
+        zero = keep.tile([P, 1], F32, name="zero")
+        nc.vector.memset(tab_sc[:].bitcast(I32), 0)
+        nc.gpsimd.memset(zero[:], 0.0)
+        nc.gpsimd.memset(w2_sc_raw[:].bitcast(I32), 0)
+        nc.gpsimd.memset(w2_sc[:].bitcast(I32), 0)
+        zero_bias = keep.tile([P, 1], F32, name="zero_bias")
+        nc.scalar.activation(zero_bias[:], zero[:], ACT.Gelu_apprx_tanh)
+
+        tab = [keep.tile([P, T], U32, name="tab%d" % a, tag="big%d" % a, align_bytes=64) for a in range(2)]
+        w1_raw = {
+            (a, b): keep.tile([P, PACK, PASS], F32, name="w1_raw%d%d" % (a, b), tag="w1_raw%d%d" % (a, b), align_bytes=64)
+            for a in range(2)
+            for b in range(2)
+        }
+        gain_sb = keep.tile([P, 2, PACK], F32, name="gain_sb")
+        w2_raw = keep.tile([P, 4 * H], U8, name="w2_raw", align_bytes=64)
+
+        def load_tab(a):
+            nc.sync.dma_start(
+                tab[a][:].bitcast(I32), tab_words[a].rearrange("p n i -> p (n i)").bitcast(I32)
+            )
+
+        def load_tab_scales(a):
+            for q in range(4):
+                nc.sync.dma_start(
+                    tab_sc[32 * q + 4 * a : 32 * q + 4 * a + 4, :].bitcast(I32),
+                    tab_scales[a, 4 * q : 4 * q + 4, :].bitcast(I32),
+                )
+
+        def load_w1(a, b):
+            rows = w1[a * PASS : (a + 1) * PASS, b * PASS : (b + 1) * PASS]
+            nc.sync.dma_start(w1_raw[a, b][:], rows.rearrange("(p j) c -> p j c", j=PACK))
+
+        nc.sync.dma_start(offs_sb[:], offs)
+        load_tab(0)
+        load_tab_scales(0)
+        load_w1(0, 0)
+        load_tab_scales(1)
+        nc.sync.dma_start(
+            w2_sc_raw[0:P:4, :].bitcast(I32), w2_scales.rearrange("a q n -> (a q) n").bitcast(I32)
+        )
+        load_tab(1)
+        nc.sync.dma_start(pos1_sb[:], pos1)
+        nc.sync.dma_start(pos2_sb[:], pos2)
+        load_w1(1, 0)
+        nc.sync.dma_start(
+            w2_raw[:].bitcast(I32).rearrange("p (a n) -> p a n", a=2),
+            w2_words.rearrange("a p n -> p a n").bitcast(I32),
+        )
+        load_w1(0, 1)
+        load_w1(1, 1)
+        nc.sync.dma_start(gain_sb[:], gain.rearrange("(b p t) -> p b t", b=2, t=PACK))
+
+        v_sc = keep.tile([P, S], U8, name="v_sc", align_bytes=64)
+        v = [keep.tile([P, S], U32, name="v%d" % a, align_bytes=64) for a in range(2)]
+
+        def gather_tab(a):
+            nc.vector.tensor_copy(v[a][:], tab[a][:].indirect(offs_sb[:]))
+
+        w1_codes = {}
+        w1_sc = {}
+
+        def quantise_w1(a, b, u, on_vector):
+            name = "%d%d%d" % (a, b, u)
+            grouped = keep.tile([P, 2, P, PACK], BF16, name="w1_bf" + name, tag="w1_bf" + name, align_bytes=64)
+            dst = grouped[:].rearrange("p t m j -> p m j t")
+            src = w1_raw[a, b][:].rearrange("p j (m t) -> p m j t", t=PACK)[:, :, :, 2 * u : 2 * u + 2]
+            if on_vector:
+                nc.vector.tensor_copy(dst, src)
+            else:
+                nc.scalar.copy(dst, src)
+            w1_codes[a, b, u] = keep.tile([P, 2 * P], U32, name="w1_codes" + name, align_bytes=64)
+            w1_sc[a, b, u] = keep.tile([P, 2 * P], U8, name="w1_sc" + name, align_bytes=64)
+            nc.vector.quantize_mx(
+                out=w1_codes[a, b, u][:].bitcast(FP8X4),
+                scales=w1_sc[a, b, u][:],
+                in_=grouped[:].rearrange("p t m j -> p (t m j)"),
+            )
+
+        h_ps = {}
+
+        def stage1_pass(a, b, t):
+            cols = slice((t % 2) * P, (t % 2 + 1) * P)
+            for half in range(2):
+                if a == 0:
+                    h_ps[b, t, half] = bank(2 * t + half, "h_ps%d%d%d" % (b, t, half))
+                picks = slice(half * BANK, (half + 1) * BANK)
+                nc.tensor.matmul_mx(
+                    out=h_ps[b, t, half][:],
+                    lhsT=w1_codes[a, b, t // 2][:, cols].bitcast(FP8X4),
+                    lhsT_scale=w1_sc[a, b, t // 2][:, cols],
+                    rhs=v[a][:, picks].bitcast(FP8X4),
+                    rhs_scale=v_sc[4 * a : P, picks],
+                    start=(a == 0),
+                    stop=(a == 1),
+                )
+
+        h = {}
+
+        def empty_h(b, t):
+            tag = "w1_raw01" if (b, t) == (0, 2) else "h%d%d" % (b, t)
+            h[b, t] = keep.tile([P, S], F32, name="h%d%d" % (b, t), tag=tag, align_bytes=64)
+            for half in range(2):
+                nc.scalar.copy(h[b, t][:, half * BANK : (half + 1) * BANK], h_ps[b, t, half][:])
+
+        hp = {}
+        hs = {}
+
+        def pick_spawning(b, t):
+            if t == 0:
+                hp[b] = keep.tile([P, PACK, E], F32, name="hp%d" % b, tag="picked%d" % b, align_bytes=64)
+            nc.vector.tensor_copy(hp[b][:, t, :], h[b, t][:].indirect(pos1_sb[:]))
+
+        def pick_settling(b, t):
+            tag = "w1_bf11%d" % (t - 2) if b == 0 and t >= 2 else "hs%d%d" % (b, t)
+            hs[b, t] = keep.tile([P, E], F32, name="hs%d%d" % (b, t), tag=tag, align_bytes=64)
+            nc.vector.tensor_copy(hs[b, t][:], h[b, t][:].indirect(pos2_sb[:]))
+
+        gather_tab(0)
+        nc.vector.tensor_copy(v_sc[:], tab_sc[:].indirect(offs_sb[:]))
+        quantise_w1(0, 0, 0, False)
+        quantise_w1(0, 0, 1, False)
+        w2_sc_rows = keep.tile([P, H], U8, name="w2_sc_rows", align_bytes=64)
+        nc.vector.tensor_copy(
+            w2_sc_rows[:].rearrange("p (b t m) -> p b t m", b=2, t=PACK),
+            w2_sc_raw[:].rearrange("p (b m t) -> p b t m", b=2, t=PACK),
+        )
+        for a in range(2):
+            for q in range(4):
+                first = 4 * (16 * a + 4 * q)
+                nc.sync.dma_start(
+                    w2_sc[32 * q : 32 * q + 4, a * H : (a + 1) * H].bitcast(I32),
+                    w2_sc_rows[first : first + 16 : 4, :].bitcast(I32),
+                )
+        for t in range(PACK):
+            stage1_pass(0, 0, t)
+        gather_tab(1)
+        quantise_w1(1, 0, 0, True)
+        quantise_w1(1, 0, 1, False)
+        for t in range(PACK):
+            stage1_pass(1, 0, t)
+
+        empty_h(0, 0)
+        w2_codes = keep.tile([P, 4 * H], U8, name="w2_codes", align_bytes=64)
+        nc.vector.tensor_copy(
+            w2_codes[:].bitcast(U16).rearrange("p (g t m) -> p g t m", g=4, t=PACK),
+            w2_raw[:].bitcast(U16).rearrange("p (g m t) -> p g t m", g=4, t=PACK),
+        )
+        pick_spawning(0, 0)
+        pick_settling(0, 0)
+        empty_h(0, 1)
+        pick_spawning(0, 1)
+        pick_settling(0, 1)
+        quantise_w1(0, 1, 0, False)
+        quantise_w1(0, 1, 1, False)
+        empty_h(0, 2)
+        pick_spawning(0, 2)
+        empty_h(0, 3)
+        pick_spawning(0, 3)
+        quantise_w1(1, 1, 0, False)
+        pick_settling(0, 2)
+        quantise_w1(1, 1, 1, False)
+        pick_settling(0, 3)
+        for a in range(2):
+            for t in range(PACK):
+                stage1_pass(a, 1, t)
+        for t in range(PACK):
+            empty_h(1, t)
+            pick_spawning(1, t)
+            pick_settling(1, t)
+
+        half_gain = keep.tile([P, 2, PACK], F32, name="half_gain")
+        nc.scalar.activation(half_gain[:], gain_sb[:], ACT.Copy, scale=0.5)
+        x_codes = []
+        x_sc = []
+        x_bf = []
+        for a in range(2):
+            tag = "w1_raw11" if a == 0 else "act1"
+            act = keep.tile([P, PACK, E], F32, name="act%d" % a, tag=tag, align_bytes=64)
+            x_bf.append(keep.tile([P, PACK, E], BF16, name="x_bf%d" % a, align_bytes=64))
+            for t in range(PACK):
+                nc.scalar.activation(act[:, t, :], hp[a][:, t, :], ACT.Gelu_apprx_tanh, bias=zero_bias[:])
+                nc.scalar.activation(
+                    x_bf[a][:, t, :], act[:, t, :], ACT.Copy, scale=half_gain[:, a, t : t + 1]
+                )
+        for a in range(2):
+            grouped = keep.tile([P, E, PACK], BF16, name="x_grouped%d" % a, align_bytes=64)
+            nc.vector.tensor_copy(
+                grouped[:].rearrange("p (c i) t -> p c t i", i=4),
+                x_bf[a][:].rearrange("p t (c i) -> p c t i", i=4),
+            )
+            x_codes.append(keep.tile([P, E], U32, name="x_codes%d" % a, align_bytes=64))
+            x_sc.append(keep.tile([P, E], U8, name="x_sc%d" % a, align_bytes=64))
+            nc.vector.quantize_mx(
+                out=x_codes[a][:].bitcast(FP8X4),
+                scales=x_sc[a][:],
+                in_=grouped[:].rearrange("p m t -> p (m t)"),
+            )
+
+        tiles = [(b, t) for b in range(2) for t in range(PACK)]
+        y_ps = {}
+        for a in range(2):
+            for b, t in tiles:
+                if a == 0:
+                    y_ps[b, t] = bank(PACK * b + t, "y_ps%d%d" % (b, t))
+                first = ((2 * a + b) * PACK + t) * P
+                nc.tensor.matmul_mx(
+                    out=y_ps[b, t][:],
+                    lhsT=w2_codes[:, 2 * first : 2 * (first + P)].bitcast(FP4X4),
+                    lhsT_scale=w2_sc[:, first : first + P],
+                    rhs=x_codes[a][:].bitcast(FP8X4),
+                    rhs_scale=x_sc[a][:],
+                    start=(a == 0),
+                    stop=(a == 1),
+                )
+
+        out_rows = out.rearrange("(b p t) m -> b t p m", b=2, t=PACK)
+        th = keep.tile([P, 2, PACK, E], F32, name="th", tag="act1", align_bytes=64)
+        gated = keep.tile([P, 2, PACK, E], F32, name="gated", tag="big1", align_bytes=64)
+
+        def gate(b, t):
+            nc.scalar.activation(th[:, b, t, :], hs[b, t][:], ACT.Tanh, bias=zero_bias[:], scale=0.5)
+            nc.vector.scalar_tensor_tensor(gated[:, b, t, :], th[:, b, t, :], 1.0, y_ps[b, t][:], ALU.add, ALU.mult)
+
+        def finish(b, t):
+            res = keep.tile([P, E], F32, name="res%d%d" % (b, t), align_bytes=64)
+            nc.vector.tensor_tensor(res[:], gated[:, b, t, :], hs[b, t][:], ALU.add)
+            nc.sync.dma_start(out_rows[b, t], res[:])
+
+        gate(*tiles[0])
+        for i in range(1, len(tiles)):
+            gate(*tiles[i])
+            finish(*tiles[i - 1])
+        finish(*tiles[-1])

@@ -29,6 +29,7 @@ def tile_list_larva_drift_step_kernel(
     with ExitStack() as ctx:
         lists = ctx.enter_context(tc.tile_pool(name="lists", bufs=1))
         keep = ctx.enter_context(tc.tile_pool(name="keep", bufs=1))
+        arena = ctx.enter_context(tc.tile_pool(name="arena", bufs=1))
         psum = ctx.enter_context(tc.psum_pool(name="psum", bufs=1))
 
         offs_sb = lists.tile([P, S // 16], U16, name="offs_sb")
@@ -38,102 +39,101 @@ def tile_list_larva_drift_step_kernel(
         def bank(i, name):
             return psum.tile([P, BANK], F32, name=name, tag="bank%d" % i)
 
+        def placed(name, shape, dtype, kib):
+            return arena.tile(shape, dtype, name=name, align_bytes=64, offset=kib * 1024)
+
         tab_sc = keep.tile([P, T], U8, name="tab_sc", align_bytes=64)
         w2_sc_raw = keep.tile([P, H], U8, name="w2_sc_raw", align_bytes=64)
         w2_sc = keep.tile([P, 2 * H], U8, name="w2_sc", align_bytes=64)
+        v_sc = [keep.tile([P, S], U8, name="v_sc%d" % a, align_bytes=64) for a in range(2)]
         zero = keep.tile([P, 1], F32, name="zero")
-        nc.vector.memset(tab_sc[:].bitcast(I32), 0)
         nc.gpsimd.memset(zero[:], 0.0)
-        nc.gpsimd.memset(w2_sc_raw[:].bitcast(I32), 0)
+        for rows in (slice(32, 64), slice(64, P)):
+            nc.vector.memset(tab_sc[rows, :].bitcast(I32), 0)
+        for rows in (slice(32, 64), slice(64, P)):
+            nc.gpsimd.memset(w2_sc_raw[rows, :].bitcast(I32), 0)
+        for a in range(2):
+            nc.gpsimd.memset(v_sc[a][:].bitcast(I32), 0)
         nc.gpsimd.memset(w2_sc[:].bitcast(I32), 0)
         zero_bias = keep.tile([P, 1], F32, name="zero_bias")
         nc.scalar.activation(zero_bias[:], zero[:], ACT.Gelu_apprx_tanh)
 
-        tab = [keep.tile([P, T], U32, name="tab%d" % a, tag="big%d" % a, align_bytes=64) for a in range(2)]
-        w1_raw = {
-            (a, b): keep.tile([P, PACK, PASS], F32, name="w1_raw%d%d" % (a, b), tag="w1_raw%d%d" % (a, b), align_bytes=64)
-            for a in range(2)
-            for b in range(2)
-        }
+        tab = [placed("tab%d" % a, [P, T], U32, 20 * a) for a in range(2)]
+        w1_raw_at = {(0, 0): 36, (1, 0): 0, (0, 1): 12, (1, 1): 24}
+        w1_raw = {}
         gain_sb = keep.tile([P, 2, PACK], F32, name="gain_sb")
-        w2_raw = keep.tile([P, 4 * H], U8, name="w2_raw", align_bytes=64)
+        half_gain = keep.tile([P, 2, PACK], F32, name="half_gain")
 
         def load_tab(a):
             nc.sync.dma_start(
                 tab[a][:].bitcast(I32), tab_words[a].rearrange("p n i -> p (n i)").bitcast(I32)
             )
 
-        def load_tab_scales(a):
-            for q in range(4):
-                nc.sync.dma_start(
-                    tab_sc[32 * q + 4 * a : 32 * q + 4 * a + 4, :].bitcast(I32),
-                    tab_scales[a, 4 * q : 4 * q + 4, :].bitcast(I32),
-                )
-
         def load_w1(a, b):
+            w1_raw[a, b] = placed("w1_raw%d%d" % (a, b), [P, PACK, PASS], F32, w1_raw_at[a, b])
             rows = w1[a * PASS : (a + 1) * PASS, b * PASS : (b + 1) * PASS]
             nc.sync.dma_start(w1_raw[a, b][:], rows.rearrange("(p j) c -> p j c", j=PACK))
 
+        nc.sync.dma_start(tab_sc[0:32, :].bitcast(I32), tab_scales.rearrange("a q n -> (a q) n").bitcast(I32))
         nc.sync.dma_start(offs_sb[:], offs)
         load_tab(0)
-        load_tab_scales(0)
-        load_w1(0, 0)
-        load_tab_scales(1)
-        nc.sync.dma_start(
-            w2_sc_raw[0:P:4, :].bitcast(I32), w2_scales.rearrange("a q n -> (a q) n").bitcast(I32)
-        )
-        load_tab(1)
+        nc.sync.dma_start(w2_sc_raw[0:32, :].bitcast(I32), w2_scales.rearrange("a q n -> (a q) n").bitcast(I32))
         nc.sync.dma_start(pos1_sb[:], pos1)
         nc.sync.dma_start(pos2_sb[:], pos2)
-        load_w1(1, 0)
-        nc.sync.dma_start(
-            w2_raw[:].bitcast(I32).rearrange("p (a n) -> p a n", a=2),
-            w2_words.rearrange("a p n -> p a n").bitcast(I32),
-        )
-        load_w1(0, 1)
-        load_w1(1, 1)
-        nc.sync.dma_start(gain_sb[:], gain.rearrange("(b p t) -> p b t", b=2, t=PACK))
+        load_w1(0, 0)
+        load_tab(1)
+        nc.gpsimd.dma_start(gain_sb[:], gain.rearrange("(b p t) -> p b t", b=2, t=PACK))
+        nc.gpsimd.tensor_scalar(half_gain[:], gain_sb[:], 0.5, 0.0, ALU.mult, ALU.add)
 
-        v_sc = keep.tile([P, S], U8, name="v_sc", align_bytes=64)
-        v = [keep.tile([P, S], U32, name="v%d" % a, align_bytes=64) for a in range(2)]
+        def to_planes(engine, plane, rows, a):
+            for r in range(4):
+                first = 16 * a + r
+                engine.dma_start(plane[r:P:32, :].bitcast(I32), rows[first : first + 13 : 4, :].bitcast(I32))
+
+        v = {}
 
         def gather_tab(a):
+            if a == 0:
+                v[a] = keep.tile([P, S], U32, name="v0", align_bytes=64)
+            else:
+                v[a] = placed("v1", [P, S], U32, 8)
             nc.vector.tensor_copy(v[a][:], tab[a][:].indirect(offs_sb[:]))
 
         w1_codes = {}
         w1_sc = {}
 
-        def quantise_w1(a, b, u, on_vector):
-            name = "%d%d%d" % (a, b, u)
-            grouped = keep.tile([P, 2, P, PACK], BF16, name="w1_bf" + name, tag="w1_bf" + name, align_bytes=64)
+        def quantise_w1(a, b, t0, nt, engine_copy, grouped):
+            name = "%d%d%d" % (a, b, t0)
             dst = grouped[:].rearrange("p t m j -> p m j t")
-            src = w1_raw[a, b][:].rearrange("p j (m t) -> p m j t", t=PACK)[:, :, :, 2 * u : 2 * u + 2]
-            if on_vector:
-                nc.vector.tensor_copy(dst, src)
-            else:
-                nc.scalar.copy(dst, src)
-            w1_codes[a, b, u] = keep.tile([P, 2 * P], U32, name="w1_codes" + name, align_bytes=64)
-            w1_sc[a, b, u] = keep.tile([P, 2 * P], U8, name="w1_sc" + name, align_bytes=64)
+            src = w1_raw[a, b][:].rearrange("p j (m t) -> p m j t", t=PACK)[:, :, :, t0 : t0 + nt]
+            engine_copy(dst, src)
+            codes = keep.tile([P, nt, P], U32, name="w1_codes" + name, align_bytes=64)
+            scales = keep.tile([P, nt, P], U8, name="w1_sc" + name, align_bytes=64)
             nc.vector.quantize_mx(
-                out=w1_codes[a, b, u][:].bitcast(FP8X4),
-                scales=w1_sc[a, b, u][:],
+                out=codes[:].rearrange("p t m -> p (t m)").bitcast(FP8X4),
+                scales=scales[:].rearrange("p t m -> p (t m)"),
                 in_=grouped[:].rearrange("p t m j -> p (t m j)"),
             )
+            for t in range(nt):
+                w1_codes[a, b, t0 + t] = codes[:, t, :]
+                w1_sc[a, b, t0 + t] = scales[:, t, :]
+
+        def pair_tile(name):
+            return keep.tile([P, 2, P, PACK], BF16, name=name, tag=name, align_bytes=64)
 
         h_ps = {}
 
         def stage1_pass(a, b, t):
-            cols = slice((t % 2) * P, (t % 2 + 1) * P)
             for half in range(2):
                 if a == 0:
                     h_ps[b, t, half] = bank(2 * t + half, "h_ps%d%d%d" % (b, t, half))
                 picks = slice(half * BANK, (half + 1) * BANK)
                 nc.tensor.matmul_mx(
                     out=h_ps[b, t, half][:],
-                    lhsT=w1_codes[a, b, t // 2][:, cols].bitcast(FP8X4),
-                    lhsT_scale=w1_sc[a, b, t // 2][:, cols],
+                    lhsT=w1_codes[a, b, t].bitcast(FP8X4),
+                    lhsT_scale=w1_sc[a, b, t],
                     rhs=v[a][:, picks].bitcast(FP8X4),
-                    rhs_scale=v_sc[4 * a : P, picks],
+                    rhs_scale=v_sc[a][:, picks],
                     start=(a == 0),
                     stop=(a == 1),
                 )
@@ -141,8 +141,10 @@ def tile_list_larva_drift_step_kernel(
         h = {}
 
         def empty_h(b, t):
-            tag = "w1_raw01" if (b, t) == (0, 2) else "h%d%d" % (b, t)
-            h[b, t] = keep.tile([P, S], F32, name="h%d%d" % (b, t), tag=tag, align_bytes=64)
+            if (b, t) == (0, 2):
+                h[b, t] = placed("h02", [P, S], F32, 12)
+            else:
+                h[b, t] = keep.tile([P, S], F32, name="h%d%d" % (b, t), align_bytes=64)
             for half in range(2):
                 nc.scalar.copy(h[b, t][:, half * BANK : (half + 1) * BANK], h_ps[b, t, half][:])
 
@@ -159,31 +161,36 @@ def tile_list_larva_drift_step_kernel(
             hs[b, t] = keep.tile([P, E], F32, name="hs%d%d" % (b, t), tag=tag, align_bytes=64)
             nc.vector.tensor_copy(hs[b, t][:], h[b, t][:].indirect(pos2_sb[:]))
 
+        v_sc_rows = keep.tile([P, S], U8, name="v_sc_rows", align_bytes=64)
+        nc.vector.tensor_copy(v_sc_rows[:], tab_sc[:].indirect(offs_sb[:]))
+        for a in range(2):
+            to_planes(nc.scalar, v_sc[a], v_sc_rows, a)
         gather_tab(0)
-        nc.vector.tensor_copy(v_sc[:], tab_sc[:].indirect(offs_sb[:]))
-        quantise_w1(0, 0, 0, False)
-        quantise_w1(0, 0, 1, False)
-        w2_sc_rows = keep.tile([P, H], U8, name="w2_sc_rows", align_bytes=64)
+        load_w1(1, 0)
+        quantise_w1(0, 0, 0, PACK, nc.vector.tensor_copy, placed("w1_bf00", [P, PACK, P, PACK], BF16, 10))
+        w2_raw = placed("w2_raw", [P, 4 * H], U8, 36)
+        nc.sync.dma_start(
+            w2_raw[:].bitcast(I32).rearrange("p (a n) -> p a n", a=2),
+            w2_words.rearrange("a p n -> p a n").bitcast(I32),
+        )
+        load_w1(0, 1)
+        for t in range(PACK):
+            stage1_pass(0, 0, t)
+        gather_tab(1)
+        load_w1(1, 1)
+        quantise_w1(1, 0, 0, 2, nc.vector.tensor_copy, placed("w1_bf100", [P, 2, P, PACK], BF16, 20))
+        quantise_w1(1, 0, 2, 2, nc.scalar.copy, pair_tile("w1_bf101"))
+        for t in range(PACK):
+            stage1_pass(1, 0, t)
+
+        empty_h(0, 0)
+        w2_sc_rows = placed("w2_sc_rows", [P, H], U8, 20)
         nc.vector.tensor_copy(
             w2_sc_rows[:].rearrange("p (b t m) -> p b t m", b=2, t=PACK),
             w2_sc_raw[:].rearrange("p (b m t) -> p b t m", b=2, t=PACK),
         )
         for a in range(2):
-            for q in range(4):
-                first = 4 * (16 * a + 4 * q)
-                nc.sync.dma_start(
-                    w2_sc[32 * q : 32 * q + 4, a * H : (a + 1) * H].bitcast(I32),
-                    w2_sc_rows[first : first + 16 : 4, :].bitcast(I32),
-                )
-        for t in range(PACK):
-            stage1_pass(0, 0, t)
-        gather_tab(1)
-        quantise_w1(1, 0, 0, True)
-        quantise_w1(1, 0, 1, False)
-        for t in range(PACK):
-            stage1_pass(1, 0, t)
-
-        empty_h(0, 0)
+            to_planes(nc.sync, w2_sc[:, a * H : (a + 1) * H], w2_sc_rows, a)
         w2_codes = keep.tile([P, 4 * H], U8, name="w2_codes", align_bytes=64)
         nc.vector.tensor_copy(
             w2_codes[:].bitcast(U16).rearrange("p (g t m) -> p g t m", g=4, t=PACK),
@@ -194,15 +201,15 @@ def tile_list_larva_drift_step_kernel(
         empty_h(0, 1)
         pick_spawning(0, 1)
         pick_settling(0, 1)
-        quantise_w1(0, 1, 0, False)
-        quantise_w1(0, 1, 1, False)
+        whole = keep.tile([P, PACK, P, PACK], BF16, name="w1_bf01", align_bytes=64)
+        quantise_w1(0, 1, 0, PACK, nc.scalar.copy, whole)
         empty_h(0, 2)
         pick_spawning(0, 2)
         empty_h(0, 3)
         pick_spawning(0, 3)
-        quantise_w1(1, 1, 0, False)
+        quantise_w1(1, 1, 0, 2, nc.scalar.copy, pair_tile("w1_bf110"))
         pick_settling(0, 2)
-        quantise_w1(1, 1, 1, False)
+        quantise_w1(1, 1, 2, 2, nc.scalar.copy, pair_tile("w1_bf111"))
         pick_settling(0, 3)
         for a in range(2):
             for t in range(PACK):
@@ -212,28 +219,28 @@ def tile_list_larva_drift_step_kernel(
             pick_spawning(1, t)
             pick_settling(1, t)
 
-        half_gain = keep.tile([P, 2, PACK], F32, name="half_gain")
-        nc.scalar.activation(half_gain[:], gain_sb[:], ACT.Copy, scale=0.5)
-        x_codes = []
-        x_sc = []
+        x_codes = {}
+        x_sc = {}
         x_bf = []
         for a in range(2):
-            tag = "w1_raw11" if a == 0 else "act1"
-            act = keep.tile([P, PACK, E], F32, name="act%d" % a, tag=tag, align_bytes=64)
+            if a == 0:
+                act = placed("act0", [P, PACK, E], F32, 24)
+            else:
+                act = keep.tile([P, PACK, E], F32, name="act1", tag="act1", align_bytes=64)
             x_bf.append(keep.tile([P, PACK, E], BF16, name="x_bf%d" % a, align_bytes=64))
             for t in range(PACK):
                 nc.scalar.activation(act[:, t, :], hp[a][:, t, :], ACT.Gelu_apprx_tanh, bias=zero_bias[:])
                 nc.scalar.activation(
                     x_bf[a][:, t, :], act[:, t, :], ACT.Copy, scale=half_gain[:, a, t : t + 1]
                 )
-        for a in range(2):
+        for a, engine_copy in ((1, nc.vector.tensor_copy), (0, nc.scalar.copy)):
             grouped = keep.tile([P, E, PACK], BF16, name="x_grouped%d" % a, align_bytes=64)
-            nc.vector.tensor_copy(
+            engine_copy(
                 grouped[:].rearrange("p (c i) t -> p c t i", i=4),
                 x_bf[a][:].rearrange("p t (c i) -> p c t i", i=4),
             )
-            x_codes.append(keep.tile([P, E], U32, name="x_codes%d" % a, align_bytes=64))
-            x_sc.append(keep.tile([P, E], U8, name="x_sc%d" % a, align_bytes=64))
+            x_codes[a] = keep.tile([P, E], U32, name="x_codes%d" % a, align_bytes=64)
+            x_sc[a] = keep.tile([P, E], U8, name="x_sc%d" % a, align_bytes=64)
             nc.vector.quantize_mx(
                 out=x_codes[a][:].bitcast(FP8X4),
                 scales=x_sc[a][:],
@@ -242,10 +249,9 @@ def tile_list_larva_drift_step_kernel(
 
         tiles = [(b, t) for b in range(2) for t in range(PACK)]
         y_ps = {}
-        for a in range(2):
-            for b, t in tiles:
-                if a == 0:
-                    y_ps[b, t] = bank(PACK * b + t, "y_ps%d%d" % (b, t))
+        for b, t in tiles:
+            y_ps[b, t] = bank(PACK * b + t, "y_ps%d%d" % (b, t))
+            for a in (1, 0):
                 first = ((2 * a + b) * PACK + t) * P
                 nc.tensor.matmul_mx(
                     out=y_ps[b, t][:],
@@ -253,13 +259,13 @@ def tile_list_larva_drift_step_kernel(
                     lhsT_scale=w2_sc[:, first : first + P],
                     rhs=x_codes[a][:].bitcast(FP8X4),
                     rhs_scale=x_sc[a][:],
-                    start=(a == 0),
-                    stop=(a == 1),
+                    start=(a == 1),
+                    stop=(a == 0),
                 )
 
         out_rows = out.rearrange("(b p t) m -> b t p m", b=2, t=PACK)
         th = keep.tile([P, 2, PACK, E], F32, name="th", tag="act1", align_bytes=64)
-        gated = keep.tile([P, 2, PACK, E], F32, name="gated", tag="big1", align_bytes=64)
+        gated = keep.tile([P, 2, PACK, E], F32, name="gated", align_bytes=64)
 
         def gate(b, t):
             nc.scalar.activation(th[:, b, t, :], hs[b, t][:], ACT.Tanh, bias=zero_bias[:], scale=0.5)
@@ -267,11 +273,11 @@ def tile_list_larva_drift_step_kernel(
 
         def finish(b, t):
             res = keep.tile([P, E], F32, name="res%d%d" % (b, t), align_bytes=64)
-            nc.vector.tensor_tensor(res[:], gated[:, b, t, :], hs[b, t][:], ALU.add)
+            engine = nc.gpsimd if b == 0 else nc.vector
+            engine.tensor_tensor(res[:], gated[:, b, t, :], hs[b, t][:], ALU.add)
             nc.sync.dma_start(out_rows[b, t], res[:])
 
-        gate(*tiles[0])
-        for i in range(1, len(tiles)):
-            gate(*tiles[i])
-            finish(*tiles[i - 1])
-        finish(*tiles[-1])
+        for b, t in tiles:
+            gate(b, t)
+        for b, t in tiles:
+            finish(b, t)

@@ -44,22 +44,19 @@ def tile_list_larva_drift_step_kernel(
 
         tab_sc = keep.tile([P, T], U8, name="tab_sc", align_bytes=64)
         w2_sc_raw = keep.tile([P, H], U8, name="w2_sc_raw", align_bytes=64)
-        w2_sc = keep.tile([P, 2 * H], U8, name="w2_sc", align_bytes=64)
-        v_sc = [keep.tile([P, S], U8, name="v_sc%d" % a, align_bytes=64) for a in range(2)]
+        v_sc = [keep.tile([P, S], U8, name="v_sc0", align_bytes=64)]
         zero = keep.tile([P, 1], F32, name="zero")
         nc.gpsimd.memset(zero[:], 0.0)
         for rows in (slice(32, 64), slice(64, P)):
             nc.vector.memset(tab_sc[rows, :].bitcast(I32), 0)
         for rows in (slice(32, 64), slice(64, P)):
             nc.gpsimd.memset(w2_sc_raw[rows, :].bitcast(I32), 0)
-        for a in range(2):
-            nc.gpsimd.memset(v_sc[a][:].bitcast(I32), 0)
-        nc.gpsimd.memset(w2_sc[:].bitcast(I32), 0)
+        nc.gpsimd.memset(v_sc[0][:].bitcast(I32), 0)
         zero_bias = keep.tile([P, 1], F32, name="zero_bias")
         nc.scalar.activation(zero_bias[:], zero[:], ACT.Gelu_apprx_tanh)
 
-        tab = [placed("tab%d" % a, [P, T], U32, 20 * a) for a in range(2)]
-        w1_raw_at = {(0, 0): 36, (1, 0): 0, (0, 1): 12, (1, 1): 24}
+        tab = [placed("tab%d" % a, [P, T], U32, 21 * a) for a in range(2)]
+        w1_raw_at = {(0, 0): 37, (1, 0): 0, (0, 1): 13, (1, 1): 25}
         w1_raw = {}
         gain_sb = keep.tile([P, 2, PACK], F32, name="gain_sb")
         half_gain = keep.tile([P, 2, PACK], F32, name="half_gain")
@@ -96,18 +93,26 @@ def tile_list_larva_drift_step_kernel(
             if a == 0:
                 v[a] = keep.tile([P, S], U32, name="v0", align_bytes=64)
             else:
-                v[a] = placed("v1", [P, S], U32, 8)
+                v[a] = placed("v1", [P, S], U32, 9)
             nc.vector.tensor_copy(v[a][:], tab[a][:].indirect(offs_sb[:]))
 
         w1_codes = {}
         w1_sc = {}
 
-        def quantise_w1(a, b, t0, nt, engine_copy, grouped):
+        def quantise_w1(a, b, t0, nt, engine_copy, grouped, codes_at=None):
             name = "%d%d%d" % (a, b, t0)
-            dst = grouped[:].rearrange("p t m j -> p m j t")
-            src = w1_raw[a, b][:].rearrange("p j (m t) -> p m j t", t=PACK)[:, :, :, t0 : t0 + nt]
-            engine_copy(dst, src)
-            codes = keep.tile([P, nt, P], U32, name="w1_codes" + name, align_bytes=64)
+            src = w1_raw[a, b][:].rearrange("p j (m t) -> p m t j", t=PACK)
+            for u in range(0, nt, 2):
+                dst = grouped[:, u : u + 2].rearrange("p t m j -> p m t j")
+                if engine_copy is gpsimd_copy:
+                    for t in range(2):
+                        engine_copy(dst[:, :, t, :], src[:, :, t0 + u + t, :])
+                else:
+                    engine_copy(dst, src[:, :, t0 + u : t0 + u + 2, :])
+            if codes_at is None:
+                codes = keep.tile([P, nt, P], U32, name="w1_codes" + name, align_bytes=64)
+            else:
+                codes = placed("w1_codes" + name, [P, nt, P], U32, codes_at)
             scales = keep.tile([P, nt, P], U8, name="w1_sc" + name, align_bytes=64)
             nc.vector.quantize_mx(
                 out=codes[:].rearrange("p t m -> p (t m)").bitcast(FP8X4),
@@ -117,6 +122,9 @@ def tile_list_larva_drift_step_kernel(
             for t in range(nt):
                 w1_codes[a, b, t0 + t] = codes[:, t, :]
                 w1_sc[a, b, t0 + t] = scales[:, t, :]
+
+        def gpsimd_copy(dst, src):
+            nc.gpsimd.tensor_scalar(dst, src, 1.0, 0.0, ALU.mult, ALU.add)
 
         def pair_tile(name):
             return keep.tile([P, 2, P, PACK], BF16, name=name, tag=name, align_bytes=64)
@@ -141,56 +149,60 @@ def tile_list_larva_drift_step_kernel(
         h = {}
 
         def empty_h(b, t):
-            if (b, t) == (0, 2):
-                h[b, t] = placed("h02", [P, S], F32, 12)
-            else:
-                h[b, t] = keep.tile([P, S], F32, name="h%d%d" % (b, t), align_bytes=64)
+            h[b, t] = keep.tile([P, S], F32, name="h%d%d" % (b, t), align_bytes=64)
             for half in range(2):
                 nc.scalar.copy(h[b, t][:, half * BANK : (half + 1) * BANK], h_ps[b, t, half][:])
 
         hp = {}
         hs = {}
 
-        def pick_spawning(b, t):
-            if t == 0:
-                hp[b] = keep.tile([P, PACK, E], F32, name="hp%d" % b, tag="picked%d" % b, align_bytes=64)
-            nc.vector.tensor_copy(hp[b][:, t, :], h[b, t][:].indirect(pos1_sb[:]))
+        def edge_tile(name, where):
+            if isinstance(where, int):
+                return placed(name, [P, E], F32, where)
+            return keep.tile([P, E], F32, name=name, tag=where or name, align_bytes=64)
 
-        def pick_settling(b, t):
-            tag = "w1_bf11%d" % (t - 2) if b == 0 and t >= 2 else "hs%d%d" % (b, t)
-            hs[b, t] = keep.tile([P, E], F32, name="hs%d%d" % (b, t), tag=tag, align_bytes=64)
+        def pick_spawning(b, t, where=None):
+            hp[b, t] = edge_tile("hp%d%d" % (b, t), where)
+            nc.vector.tensor_copy(hp[b, t][:], h[b, t][:].indirect(pos1_sb[:]))
+
+        def pick_settling(b, t, where=None):
+            hs[b, t] = edge_tile("hs%d%d" % (b, t), where)
             nc.vector.tensor_copy(hs[b, t][:], h[b, t][:].indirect(pos2_sb[:]))
 
         v_sc_rows = keep.tile([P, S], U8, name="v_sc_rows", align_bytes=64)
         nc.vector.tensor_copy(v_sc_rows[:], tab_sc[:].indirect(offs_sb[:]))
-        for a in range(2):
-            to_planes(nc.scalar, v_sc[a], v_sc_rows, a)
+        to_planes(nc.scalar, v_sc[0], v_sc_rows, 0)
         gather_tab(0)
         load_w1(1, 0)
-        quantise_w1(0, 0, 0, PACK, nc.vector.tensor_copy, placed("w1_bf00", [P, PACK, P, PACK], BF16, 10))
-        w2_raw = placed("w2_raw", [P, 4 * H], U8, 36)
+        v_sc.append(placed("v_sc1", [P, S], U8, 8))
+        nc.gpsimd.memset(v_sc[1][:].bitcast(I32), 0)
+        to_planes(nc.scalar, v_sc[1], v_sc_rows, 1)
+        quantise_w1(0, 0, 0, PACK, nc.vector.tensor_copy, placed("w1_bf00", [P, PACK, P, PACK], BF16, 11))
+        w2_raw = placed("w2_raw", [P, 4 * H], U8, 37)
         nc.sync.dma_start(
             w2_raw[:].bitcast(I32).rearrange("p (a n) -> p a n", a=2),
             w2_words.rearrange("a p n -> p a n").bitcast(I32),
         )
         load_w1(0, 1)
+        w2_sc_rows = placed("w2_sc_rows", [P, H], U8, 41)
+        nc.vector.tensor_copy(
+            w2_sc_rows[:].rearrange("p (b t m) -> p b t m", b=2, t=PACK),
+            w2_sc_raw[:].rearrange("p (b m t) -> p b t m", b=2, t=PACK),
+        )
         for t in range(PACK):
             stage1_pass(0, 0, t)
         gather_tab(1)
         load_w1(1, 1)
-        quantise_w1(1, 0, 0, 2, nc.vector.tensor_copy, placed("w1_bf100", [P, 2, P, PACK], BF16, 20))
+        w2_sc = placed("w2_sc", [P, 2 * H], U8, 33)
+        nc.gpsimd.memset(w2_sc[:].bitcast(I32), 0)
+        for a in range(2):
+            to_planes(nc.sync, w2_sc[:, a * H : (a + 1) * H], w2_sc_rows, a)
+        quantise_w1(1, 0, 0, 2, nc.vector.tensor_copy, placed("w1_bf100", [P, 2, P, PACK], BF16, 21))
         quantise_w1(1, 0, 2, 2, nc.scalar.copy, pair_tile("w1_bf101"))
         for t in range(PACK):
             stage1_pass(1, 0, t)
 
         empty_h(0, 0)
-        w2_sc_rows = placed("w2_sc_rows", [P, H], U8, 20)
-        nc.vector.tensor_copy(
-            w2_sc_rows[:].rearrange("p (b t m) -> p b t m", b=2, t=PACK),
-            w2_sc_raw[:].rearrange("p (b m t) -> p b t m", b=2, t=PACK),
-        )
-        for a in range(2):
-            to_planes(nc.sync, w2_sc[:, a * H : (a + 1) * H], w2_sc_rows, a)
         w2_codes = keep.tile([P, 4 * H], U8, name="w2_codes", align_bytes=64)
         nc.vector.tensor_copy(
             w2_codes[:].bitcast(U16).rearrange("p (g t m) -> p g t m", g=4, t=PACK),
@@ -198,60 +210,70 @@ def tile_list_larva_drift_step_kernel(
         )
         pick_spawning(0, 0)
         pick_settling(0, 0)
+        pair = [P, 2, P, PACK]
+        quantise_w1(0, 1, 0, 2, gpsimd_copy, placed("w1_bf010", pair, BF16, 46))
         empty_h(0, 1)
-        pick_spawning(0, 1)
-        pick_settling(0, 1)
-        whole = keep.tile([P, PACK, P, PACK], BF16, name="w1_bf01", align_bytes=64)
-        quantise_w1(0, 1, 0, PACK, nc.scalar.copy, whole)
+        pick_spawning(0, 1, 45)
+        pick_settling(0, 1, 47)
         empty_h(0, 2)
-        pick_spawning(0, 2)
         empty_h(0, 3)
-        pick_spawning(0, 3)
-        quantise_w1(1, 1, 0, 2, nc.scalar.copy, pair_tile("w1_bf110"))
-        pick_settling(0, 2)
-        quantise_w1(1, 1, 2, 2, nc.scalar.copy, pair_tile("w1_bf111"))
-        pick_settling(0, 3)
-        for a in range(2):
-            for t in range(PACK):
-                stage1_pass(a, 1, t)
+        quantise_w1(1, 1, 0, 2, nc.scalar.copy, placed("w1_bf110", pair, BF16, 49))
+        pick_spawning(0, 2, 50)
+        quantise_w1(0, 1, 2, 2, gpsimd_copy, placed("w1_bf012", pair, BF16, 52), 49)
+        quantise_w1(1, 1, 2, 2, nc.scalar.copy, placed("w1_bf112", pair, BF16, 54))
+        pick_spawning(0, 3, 53)
         for t in range(PACK):
-            empty_h(1, t)
-            pick_spawning(1, t)
-            pick_settling(1, t)
+            for a in range(2):
+                stage1_pass(a, 1, t)
+
+        x_bf = [
+            keep.tile([P, PACK, E], BF16, name="x_bf%d" % a, tag="x_bf%d" % a, align_bytes=64) for a in range(2)
+        ]
+
+        def activate(a, t):
+            act = edge_tile("act%d%d" % (a, t), 25 + 2 * t if a == 0 else None)
+            nc.scalar.activation(act[:], hp[a, t][:], ACT.Gelu_apprx_tanh, bias=zero_bias[:])
+            nc.gpsimd.tensor_scalar(x_bf[a][:, t, :], act[:], half_gain[:, a, t : t + 1], 0.0, ALU.mult, ALU.add)
+
+        for t0 in (0, 2):
+            for t in (t0, t0 + 1):
+                empty_h(1, t)
+                pick_spawning(1, t)
+            for t in (t0, t0 + 1):
+                activate(0, t)
+        for t in range(PACK):
+            activate(1, t)
+        pick_settling(0, 2, "hp10")
+        pick_settling(0, 3, "hp11")
+        pick_settling(1, 0, "hp12")
+        pick_settling(1, 1, "hp13")
 
         x_codes = {}
         x_sc = {}
-        x_bf = []
-        for a in range(2):
-            if a == 0:
-                act = placed("act0", [P, PACK, E], F32, 24)
-            else:
-                act = keep.tile([P, PACK, E], F32, name="act1", tag="act1", align_bytes=64)
-            x_bf.append(keep.tile([P, PACK, E], BF16, name="x_bf%d" % a, align_bytes=64))
-            for t in range(PACK):
-                nc.scalar.activation(act[:, t, :], hp[a][:, t, :], ACT.Gelu_apprx_tanh, bias=zero_bias[:])
-                nc.scalar.activation(
-                    x_bf[a][:, t, :], act[:, t, :], ACT.Copy, scale=half_gain[:, a, t : t + 1]
-                )
-        for a, engine_copy in ((1, nc.vector.tensor_copy), (0, nc.scalar.copy)):
-            grouped = keep.tile([P, E, PACK], BF16, name="x_grouped%d" % a, align_bytes=64)
+        x_grouped = {}
+        for a, engine_copy in ((0, nc.vector.tensor_copy), (1, nc.scalar.copy)):
+            x_grouped[a] = keep.tile(
+                [P, E, PACK], BF16, name="x_grouped%d" % a, tag="x_grouped%d" % a, align_bytes=64
+            )
             engine_copy(
-                grouped[:].rearrange("p (c i) t -> p c t i", i=4),
+                x_grouped[a][:].rearrange("p (c i) t -> p c t i", i=4),
                 x_bf[a][:].rearrange("p t (c i) -> p c t i", i=4),
             )
+        for a in range(2):
             x_codes[a] = keep.tile([P, E], U32, name="x_codes%d" % a, align_bytes=64)
             x_sc[a] = keep.tile([P, E], U8, name="x_sc%d" % a, align_bytes=64)
             nc.vector.quantize_mx(
                 out=x_codes[a][:].bitcast(FP8X4),
                 scales=x_sc[a][:],
-                in_=grouped[:].rearrange("p m t -> p (m t)"),
+                in_=x_grouped[a][:].rearrange("p m t -> p (m t)"),
             )
+        pick_settling(1, 2, "x_grouped1")
 
         tiles = [(b, t) for b in range(2) for t in range(PACK)]
         y_ps = {}
         for b, t in tiles:
             y_ps[b, t] = bank(PACK * b + t, "y_ps%d%d" % (b, t))
-            for a in (1, 0):
+            for a in range(2):
                 first = ((2 * a + b) * PACK + t) * P
                 nc.tensor.matmul_mx(
                     out=y_ps[b, t][:],
@@ -259,25 +281,34 @@ def tile_list_larva_drift_step_kernel(
                     lhsT_scale=w2_sc[:, first : first + P],
                     rhs=x_codes[a][:].bitcast(FP8X4),
                     rhs_scale=x_sc[a][:],
-                    start=(a == 1),
-                    stop=(a == 0),
+                    start=(a == 0),
+                    stop=(a == 1),
                 )
 
         out_rows = out.rearrange("(b p t) m -> b t p m", b=2, t=PACK)
-        th = keep.tile([P, 2, PACK, E], F32, name="th", tag="act1", align_bytes=64)
         gated = keep.tile([P, 2, PACK, E], F32, name="gated", align_bytes=64)
+        first_th = keep.tile([P, 2, E], F32, name="first_th", tag="x_bf0", align_bytes=64)
 
-        def gate(b, t):
-            nc.scalar.activation(th[:, b, t, :], hs[b, t][:], ACT.Tanh, bias=zero_bias[:], scale=0.5)
-            nc.vector.scalar_tensor_tensor(gated[:, b, t, :], th[:, b, t, :], 1.0, y_ps[b, t][:], ALU.add, ALU.mult)
+        def gate(i):
+            b, t = tiles[i]
+            if i < 2:
+                th = first_th[:, i, :]
+            else:
+                th = edge_tile("th%d" % i, "act1%d" % (i - 2) if i < 6 else None)[:]
+            nc.scalar.activation(th, hs[b, t][:], ACT.Tanh, bias=zero_bias[:], scale=0.5)
+            nc.vector.scalar_tensor_tensor(gated[:, b, t, :], th, 1.0, y_ps[b, t][:], ALU.add, ALU.mult)
 
-        def finish(b, t):
+        def finish(i):
+            b, t = tiles[i]
             res = keep.tile([P, E], F32, name="res%d%d" % (b, t), align_bytes=64)
-            engine = nc.gpsimd if b == 0 else nc.vector
+            engine = nc.gpsimd if i < 5 else nc.vector
             engine.tensor_tensor(res[:], gated[:, b, t, :], hs[b, t][:], ALU.add)
             nc.sync.dma_start(out_rows[b, t], res[:])
 
-        for b, t in tiles:
-            gate(b, t)
-        for b, t in tiles:
-            finish(b, t)
+        gate(0)
+        gate(1)
+        pick_settling(1, 3, "x_bf0")
+        for i in range(2, len(tiles)):
+            gate(i)
+        for i in range(len(tiles)):
+            finish(i)

@@ -227,7 +227,8 @@ def tile_list_larva_drift_step_kernel(
                 stage1_pass(a, 1, t)
 
         x_bf = [
-            keep.tile([P, PACK, E], BF16, name="x_bf%d" % a, tag="x_bf%d" % a, align_bytes=64) for a in range(2)
+            keep.tile([P, PACK, E], BF16, name="x_bf0", align_bytes=64),
+            placed("x_bf1", [P, PACK, E], BF16, 58),
         ]
 
         def activate(a, t):
@@ -243,37 +244,38 @@ def tile_list_larva_drift_step_kernel(
                 activate(0, t)
         for t in range(PACK):
             activate(1, t)
-        pick_settling(0, 2, "hp10")
-        pick_settling(0, 3, "hp11")
-        pick_settling(1, 0, "hp12")
-        pick_settling(1, 1, "hp13")
 
         x_codes = {}
         x_sc = {}
-        x_grouped = {}
-        for a, engine_copy in ((0, nc.vector.tensor_copy), (1, nc.scalar.copy)):
-            x_grouped[a] = keep.tile(
-                [P, E, PACK], BF16, name="x_grouped%d" % a, tag="x_grouped%d" % a, align_bytes=64
-            )
+
+        def quantise_x(a, engine_copy):
+            grouped = keep.tile([P, E, PACK], BF16, name="x_grouped%d" % a, tag="x_grouped%d" % a, align_bytes=64)
             engine_copy(
-                x_grouped[a][:].rearrange("p (c i) t -> p c t i", i=4),
+                grouped[:].rearrange("p (c i) t -> p c t i", i=4),
                 x_bf[a][:].rearrange("p t (c i) -> p c t i", i=4),
             )
-        for a in range(2):
             x_codes[a] = keep.tile([P, E], U32, name="x_codes%d" % a, align_bytes=64)
             x_sc[a] = keep.tile([P, E], U8, name="x_sc%d" % a, align_bytes=64)
             nc.vector.quantize_mx(
                 out=x_codes[a][:].bitcast(FP8X4),
                 scales=x_sc[a][:],
-                in_=x_grouped[a][:].rearrange("p m t -> p (m t)"),
+                in_=grouped[:].rearrange("p m t -> p (m t)"),
             )
+
+        quantise_x(0, nc.vector.tensor_copy)
+        pick_settling(0, 2, "hp10")
+        pick_settling(0, 3, "hp11")
+        pick_settling(1, 0, "hp12")
+        pick_settling(1, 1, "hp13")
+        quantise_x(1, nc.scalar.copy)
         pick_settling(1, 2, "x_grouped1")
 
         tiles = [(b, t) for b in range(2) for t in range(PACK)]
         y_ps = {}
-        for b, t in tiles:
-            y_ps[b, t] = bank(PACK * b + t, "y_ps%d%d" % (b, t))
-            for a in range(2):
+        for a in range(2):
+            for b, t in tiles:
+                if a == 0:
+                    y_ps[b, t] = bank(PACK * b + t, "y_ps%d%d" % (b, t))
                 first = ((2 * a + b) * PACK + t) * P
                 nc.tensor.matmul_mx(
                     out=y_ps[b, t][:],
@@ -287,27 +289,39 @@ def tile_list_larva_drift_step_kernel(
 
         out_rows = out.rearrange("(b p t) m -> b t p m", b=2, t=PACK)
         gated = keep.tile([P, 2, PACK, E], F32, name="gated", align_bytes=64)
-        first_th = keep.tile([P, 2, E], F32, name="first_th", tag="x_bf0", align_bytes=64)
+        first_th = placed("first_th", [P, 2, E], F32, 56)
+        later_th = placed("later_th", [P, 6, E], F32, 60)
 
         def gate(i):
             b, t = tiles[i]
             if i < 2:
                 th = first_th[:, i, :]
             else:
-                th = edge_tile("th%d" % i, "act1%d" % (i - 2) if i < 6 else None)[:]
+                th = later_th[:, i - 2, :]
             nc.scalar.activation(th, hs[b, t][:], ACT.Tanh, bias=zero_bias[:], scale=0.5)
             nc.vector.scalar_tensor_tensor(gated[:, b, t, :], th, 1.0, y_ps[b, t][:], ALU.add, ALU.mult)
 
         def finish(i):
             b, t = tiles[i]
             res = keep.tile([P, E], F32, name="res%d%d" % (b, t), align_bytes=64)
-            engine = nc.gpsimd if i < 5 else nc.vector
-            engine.tensor_tensor(res[:], gated[:, b, t, :], hs[b, t][:], ALU.add)
+            halves = [slice(0, E // 2), slice(E // 2, E)]
+            if i < 4:
+                nc.gpsimd.tensor_tensor(res[:], gated[:, b, t, :], hs[b, t][:], ALU.add)
+            elif i == 4:
+                for engine, cols in zip((nc.gpsimd, nc.vector), halves):
+                    engine.tensor_tensor(res[:, cols], gated[:, b, t, cols], hs[b, t][:, cols], ALU.add)
+            elif i < 7:
+                nc.vector.tensor_tensor(res[:], gated[:, b, t, :], hs[b, t][:], ALU.add)
+            else:
+                for cols in halves:
+                    nc.vector.tensor_tensor(res[:, cols], gated[:, b, t, cols], hs[b, t][:, cols], ALU.add)
+                    nc.sync.dma_start(out_rows[b, t][:, cols], res[:, cols])
+                return
             nc.sync.dma_start(out_rows[b, t], res[:])
 
         gate(0)
         gate(1)
-        pick_settling(1, 3, "x_bf0")
+        pick_settling(1, 3, 58)
         for i in range(2, len(tiles)):
             gate(i)
         for i in range(len(tiles)):

@@ -194,7 +194,7 @@ def tile_list_larva_drift_step_kernel(
         gather_tab(1)
         load_w1(1, 1)
         w2_sc = placed("w2_sc", [P, 2 * H], U8, 33)
-        nc.gpsimd.memset(w2_sc[:].bitcast(I32), 0)
+        nc.vector.memset(w2_sc[:].bitcast(I32), 0)
         for a in range(2):
             to_planes(nc.sync, w2_sc[:, a * H : (a + 1) * H], w2_sc_rows, a)
         quantise_w1(1, 0, 0, 2, nc.vector.tensor_copy, placed("w1_bf100", [P, 2, P, PACK], BF16, 21))
@@ -211,30 +211,35 @@ def tile_list_larva_drift_step_kernel(
         pick_spawning(0, 0)
         pick_settling(0, 0)
         pair = [P, 2, P, PACK]
-        quantise_w1(0, 1, 0, 2, gpsimd_copy, placed("w1_bf010", pair, BF16, 46))
+        wide = placed("w1_bf010", [P, 6, P, PACK], BF16, 45)
+        quantise_w1(0, 1, 0, 2, gpsimd_copy, wide[:, 0:2])
         empty_h(0, 1)
         pick_spawning(0, 1, 45)
         pick_settling(0, 1, 47)
         empty_h(0, 2)
         empty_h(0, 3)
-        quantise_w1(1, 1, 0, 2, nc.scalar.copy, placed("w1_bf110", pair, BF16, 49))
-        pick_spawning(0, 2, 50)
-        quantise_w1(0, 1, 2, 2, gpsimd_copy, placed("w1_bf012", pair, BF16, 52), 49)
-        quantise_w1(1, 1, 2, 2, nc.scalar.copy, placed("w1_bf112", pair, BF16, 54))
-        pick_spawning(0, 3, 53)
+        quantise_w1(1, 1, 0, 2, nc.scalar.copy, placed("w1_bf110", pair, BF16, 53))
+        pick_spawning(0, 2, 54)
+        quantise_w1(0, 1, 2, 2, gpsimd_copy, placed("w1_bf012", pair, BF16, 49), 53)
+        quantise_w1(1, 1, 2, 2, nc.scalar.copy, placed("w1_bf112", pair, BF16, 51))
+        pick_spawning(0, 3, 50)
         for t in range(PACK):
             for a in range(2):
                 stage1_pass(a, 1, t)
 
         x_bf = [
-            keep.tile([P, PACK, E], BF16, name="x_bf0", align_bytes=64),
-            placed("x_bf1", [P, PACK, E], BF16, 58),
+            placed("x_bf0", [P, PACK, E], BF16, 56),
+            keep.tile([P, PACK, E], BF16, name="x_bf1", align_bytes=64),
         ]
 
         def activate(a, t):
             act = edge_tile("act%d%d" % (a, t), 25 + 2 * t if a == 0 else None)
             nc.scalar.activation(act[:], hp[a, t][:], ACT.Gelu_apprx_tanh, bias=zero_bias[:])
-            nc.gpsimd.tensor_scalar(x_bf[a][:, t, :], act[:], half_gain[:, a, t : t + 1], 0.0, ALU.mult, ALU.add)
+            factor = half_gain[:, a, t : t + 1]
+            if (a, t) == (1, 3):
+                nc.scalar.activation(x_bf[a][:, t, :], act[:], ACT.Copy, scale=factor)
+            else:
+                nc.gpsimd.tensor_scalar(x_bf[a][:, t, :], act[:], factor, 0.0, ALU.mult, ALU.add)
 
         for t0 in (0, 2):
             for t in (t0, t0 + 1):
@@ -249,7 +254,7 @@ def tile_list_larva_drift_step_kernel(
         x_sc = {}
 
         def quantise_x(a, engine_copy):
-            grouped = keep.tile([P, E, PACK], BF16, name="x_grouped%d" % a, tag="x_grouped%d" % a, align_bytes=64)
+            grouped = keep.tile([P, E, PACK], BF16, name="x_grouped%d" % a, tag=("act13", "x_grouped1")[a], align_bytes=64)
             engine_copy(
                 grouped[:].rearrange("p (c i) t -> p c t i", i=4),
                 x_bf[a][:].rearrange("p t (c i) -> p c t i", i=4),
@@ -262,20 +267,18 @@ def tile_list_larva_drift_step_kernel(
                 in_=grouped[:].rearrange("p m t -> p (m t)"),
             )
 
-        quantise_x(0, nc.vector.tensor_copy)
         pick_settling(0, 2, "hp10")
         pick_settling(0, 3, "hp11")
         pick_settling(1, 0, "hp12")
-        pick_settling(1, 1, "hp13")
-        quantise_x(1, nc.scalar.copy)
-        pick_settling(1, 2, "x_grouped1")
+        quantise_x(1, nc.vector.tensor_copy)
+        quantise_x(0, nc.scalar.copy)
+        pick_settling(1, 1, "act13")
 
         tiles = [(b, t) for b in range(2) for t in range(PACK)]
         y_ps = {}
-        for a in range(2):
-            for b, t in tiles:
-                if a == 0:
-                    y_ps[b, t] = bank(PACK * b + t, "y_ps%d%d" % (b, t))
+        for b, t in tiles:
+            y_ps[b, t] = bank(PACK * b + t, "y_ps%d%d" % (b, t))
+            for a in range(2):
                 first = ((2 * a + b) * PACK + t) * P
                 nc.tensor.matmul_mx(
                     out=y_ps[b, t][:],
@@ -290,14 +293,17 @@ def tile_list_larva_drift_step_kernel(
         out_rows = out.rearrange("(b p t) m -> b t p m", b=2, t=PACK)
         gated = keep.tile([P, 2, PACK, E], F32, name="gated", align_bytes=64)
         first_th = placed("first_th", [P, 2, E], F32, 56)
-        later_th = placed("later_th", [P, 6, E], F32, 60)
+        second_th = placed("second_th", [P, 2, E], F32, 60)
+        later_th = keep.tile([P, 4, E], F32, name="later_th", align_bytes=64)
 
         def gate(i):
             b, t = tiles[i]
             if i < 2:
                 th = first_th[:, i, :]
+            elif i < 4:
+                th = second_th[:, i - 2, :]
             else:
-                th = later_th[:, i - 2, :]
+                th = later_th[:, i - 4, :]
             nc.scalar.activation(th, hs[b, t][:], ACT.Tanh, bias=zero_bias[:], scale=0.5)
             nc.vector.scalar_tensor_tensor(gated[:, b, t, :], th, 1.0, y_ps[b, t][:], ALU.add, ALU.mult)
 
@@ -305,11 +311,8 @@ def tile_list_larva_drift_step_kernel(
             b, t = tiles[i]
             res = keep.tile([P, E], F32, name="res%d%d" % (b, t), align_bytes=64)
             halves = [slice(0, E // 2), slice(E // 2, E)]
-            if i < 4:
+            if i < 5:
                 nc.gpsimd.tensor_tensor(res[:], gated[:, b, t, :], hs[b, t][:], ALU.add)
-            elif i == 4:
-                for engine, cols in zip((nc.gpsimd, nc.vector), halves):
-                    engine.tensor_tensor(res[:, cols], gated[:, b, t, cols], hs[b, t][:, cols], ALU.add)
             elif i < 7:
                 nc.vector.tensor_tensor(res[:], gated[:, b, t, :], hs[b, t][:], ALU.add)
             else:
@@ -321,8 +324,11 @@ def tile_list_larva_drift_step_kernel(
 
         gate(0)
         gate(1)
-        pick_settling(1, 3, 58)
-        for i in range(2, len(tiles)):
+        pick_settling(1, 2, 56)
+        gate(2)
+        gate(3)
+        pick_settling(1, 3, 60)
+        for i in range(4, len(tiles)):
             gate(i)
         for i in range(len(tiles)):
             finish(i)

from contextlib import ExitStack

import concourse.mybir as mybir

K, H, T, S, E = 1024, 1024, 4096, 1024, 512
FLOPS = 2 * K * H * S + 2 * H * H * E

F32 = mybir.dt.float32
BF16 = mybir.dt.bfloat16
I32 = mybir.dt.int32
U32 = mybir.dt.uint32
U16 = mybir.dt.uint16
U8 = mybir.dt.uint8
FP8X4 = mybir.dt.float8_e4m3fn_x4
FP4X4 = mybir.dt.float4_e2m1fn_x4
ALU = mybir.AluOpType
ACT = mybir.ActivationFunctionType

P = 128
PACK = 4
PASS = P * PACK
BANK = 512


def tile_list_larva_drift_step_kernel(
    tc, tab_words, tab_scales, offs, w1, pos1, pos2, gain, w2_words, w2_scales, out
):
    nc = tc.nc
    with ExitStack() as ctx:
        lists = ctx.enter_context(tc.tile_pool(name="lists", bufs=1))
        keep = ctx.enter_context(tc.tile_pool(name="keep", bufs=1))
        arena = ctx.enter_context(tc.tile_pool(name="arena", bufs=1))
        psum = ctx.enter_context(tc.psum_pool(name="psum", bufs=1))

        offs_sb = lists.tile([P, S // 16], U16, name="offs_sb")
        pos1_sb = lists.tile([P, E // 16], U16, name="pos1_sb")
        pos2_sb = lists.tile([P, E // 16], U16, name="pos2_sb")

        def bank(i, name):
            return psum.tile([P, BANK], F32, name=name, tag="bank%d" % i)

        def placed(name, shape, dtype, kib):
            return arena.tile(shape, dtype, name=name, align_bytes=64, offset=kib * 1024)

        tab_sc = keep.tile([P, T], U8, name="tab_sc", align_bytes=64)
        w2_sc_raw = keep.tile([P, H], U8, name="w2_sc_raw", align_bytes=64)
        v_sc = [keep.tile([P, S], U8, name="v_sc0", align_bytes=64)]
        zero = keep.tile([P, 1], F32, name="zero")
        nc.gpsimd.memset(zero[:], 0.0)
        for rows in (slice(32, 64), slice(64, P)):
            nc.vector.memset(tab_sc[rows, :].bitcast(I32), 0)
        for rows in (slice(32, 64), slice(64, P)):
            nc.gpsimd.memset(w2_sc_raw[rows, :].bitcast(I32), 0)
        nc.gpsimd.memset(v_sc[0][:].bitcast(I32), 0)
        zero_bias = keep.tile([P, 1], F32, name="zero_bias")
        nc.scalar.activation(zero_bias[:], zero[:], ACT.Gelu_apprx_tanh)

        tab = [placed("tab%d" % a, [P, T], U32, 21 * a) for a in range(2)]
        w1_raw_at = {(0, 0): 37, (1, 0): 0, (0, 1): 13, (1, 1): 25}
        w1_raw = {}
        gain_sb = keep.tile([P, 2, PACK], F32, name="gain_sb")
        half_gain = keep.tile([P, 2, PACK], F32, name="half_gain")

        def load_tab(a):
            nc.sync.dma_start(
                tab[a][:].bitcast(I32), tab_words[a].rearrange("p n i -> p (n i)").bitcast(I32)
            )

        def load_w1(a, b):
            w1_raw[a, b] = placed("w1_raw%d%d" % (a, b), [P, PACK, PASS], F32, w1_raw_at[a, b])
            rows = w1[a * PASS : (a + 1) * PASS, b * PASS : (b + 1) * PASS]
            nc.sync.dma_start(w1_raw[a, b][:], rows.rearrange("(p j) c -> p j c", j=PACK))

        nc.sync.dma_start(tab_sc[0:32, :].bitcast(I32), tab_scales.rearrange("a q n -> (a q) n").bitcast(I32))
        nc.sync.dma_start(offs_sb[:], offs)
        load_tab(0)
        nc.sync.dma_start(w2_sc_raw[0:32, :].bitcast(I32), w2_scales.rearrange("a q n -> (a q) n").bitcast(I32))
        nc.sync.dma_start(pos1_sb[:], pos1)
        nc.sync.dma_start(pos2_sb[:], pos2)
        load_w1(0, 0)
        load_tab(1)
        nc.gpsimd.dma_start(gain_sb[:], gain.rearrange("(b p t) -> p b t", b=2, t=PACK))
        nc.gpsimd.tensor_scalar(half_gain[:], gain_sb[:], 0.5, 0.0, ALU.mult, ALU.add)

        def to_planes(engine, plane, rows, a):
            for r in range(4):
                first = 16 * a + r
                engine.dma_start(plane[r:P:32, :].bitcast(I32), rows[first : first + 13 : 4, :].bitcast(I32))

        v = {}

        def gather_tab(a):
            if a == 0:
                v[a] = keep.tile([P, S], U32, name="v0", align_bytes=64)
            else:
                v[a] = placed("v1", [P, S], U32, 9)
            nc.vector.tensor_copy(v[a][:], tab[a][:].indirect(offs_sb[:]))

        w1_codes = {}
        w1_sc = {}

        def quantise_w1(a, b, t0, nt, engine_copy, grouped, codes_at=None):
            name = "%d%d%d" % (a, b, t0)
            src = w1_raw[a, b][:].rearrange("p j (m t) -> p m t j", t=PACK)
            for u in range(0, nt, 2):
                dst = grouped[:, u : u + 2].rearrange("p t m j -> p m t j")
                if engine_copy is gpsimd_copy:
                    for t in range(2):
                        engine_copy(dst[:, :, t, :], src[:, :, t0 + u + t, :])
                else:
                    engine_copy(dst, src[:, :, t0 + u : t0 + u + 2, :])
            if codes_at is None:
                codes = keep.tile([P, nt, P], U32, name="w1_codes" + name, align_bytes=64)
            else:
                codes = placed("w1_codes" + name, [P, nt, P], U32, codes_at)
            scales = keep.tile([P, nt, P], U8, name="w1_sc" + name, align_bytes=64)
            nc.vector.quantize_mx(
                out=codes[:].rearrange("p t m -> p (t m)").bitcast(FP8X4),
                scales=scales[:].rearrange("p t m -> p (t m)"),
                in_=grouped[:].rearrange("p t m j -> p (t m j)"),
            )
            for t in range(nt):
                w1_codes[a, b, t0 + t] = codes[:, t, :]
                w1_sc[a, b, t0 + t] = scales[:, t, :]

        def gpsimd_copy(dst, src):
            nc.gpsimd.tensor_scalar(dst, src, 1.0, 0.0, ALU.mult, ALU.add)

        def pair_tile(name):
            return keep.tile([P, 2, P, PACK], BF16, name=name, tag=name, align_bytes=64)

        h_ps = {}

        def stage1_pass(a, b, t):
            for half in range(2):
                if a == 0:
                    h_ps[b, t, half] = bank(2 * t + half, "h_ps%d%d%d" % (b, t, half))
                picks = slice(half * BANK, (half + 1) * BANK)
                nc.tensor.matmul_mx(
                    out=h_ps[b, t, half][:],
                    lhsT=w1_codes[a, b, t].bitcast(FP8X4),
                    lhsT_scale=w1_sc[a, b, t],
                    rhs=v[a][:, picks].bitcast(FP8X4),
                    rhs_scale=v_sc[a][:, picks],
                    start=(a == 0),
                    stop=(a == 1),
                )

        h = {}

        def empty_h(b, t):
            h[b, t] = keep.tile([P, S], F32, name="h%d%d" % (b, t), align_bytes=64)
            for half in range(2):
                nc.scalar.copy(h[b, t][:, half * BANK : (half + 1) * BANK], h_ps[b, t, half][:])

        hp = {}
        hs = {}

        def edge_tile(name, where):
            if isinstance(where, int):
                return placed(name, [P, E], F32, where)
            return keep.tile([P, E], F32, name=name, tag=where or name, align_bytes=64)

        def pick_spawning(b, t, where=None):
            hp[b, t] = edge_tile("hp%d%d" % (b, t), where)
            nc.vector.tensor_copy(hp[b, t][:], h[b, t][:].indirect(pos1_sb[:]))

        def pick_settling(b, t, where=None):
            hs[b, t] = edge_tile("hs%d%d" % (b, t), where)
            nc.vector.tensor_copy(hs[b, t][:], h[b, t][:].indirect(pos2_sb[:]))

        v_sc_rows = keep.tile([P, S], U8, name="v_sc_rows", align_bytes=64)
        nc.vector.tensor_copy(v_sc_rows[:], tab_sc[:].indirect(offs_sb[:]))
        to_planes(nc.scalar, v_sc[0], v_sc_rows, 0)
        gather_tab(0)
        load_w1(1, 0)
        v_sc.append(placed("v_sc1", [P, S], U8, 8))
        nc.gpsimd.memset(v_sc[1][:].bitcast(I32), 0)
        to_planes(nc.scalar, v_sc[1], v_sc_rows, 1)
        quantise_w1(0, 0, 0, PACK, nc.vector.tensor_copy, placed("w1_bf00", [P, PACK, P, PACK], BF16, 11))
        w2_raw = placed("w2_raw", [P, 4 * H], U8, 37)
        nc.sync.dma_start(
            w2_raw[:].bitcast(I32).rearrange("p (a n) -> p a n", a=2),
            w2_words.rearrange("a p n -> p a n").bitcast(I32),
        )
        load_w1(0, 1)
        w2_sc_rows = placed("w2_sc_rows", [P, H], U8, 41)
        nc.vector.tensor_copy(
            w2_sc_rows[:].rearrange("p (b t m) -> p b t m", b=2, t=PACK),
            w2_sc_raw[:].rearrange("p (b m t) -> p b t m", b=2, t=PACK),
        )
        for t in range(PACK):
            stage1_pass(0, 0, t)
        gather_tab(1)
        load_w1(1, 1)
        w2_sc = placed("w2_sc", [P, 2 * H], U8, 33)
        nc.vector.memset(w2_sc[:].bitcast(I32), 0)
        for a in range(2):
            to_planes(nc.sync, w2_sc[:, a * H : (a + 1) * H], w2_sc_rows, a)
        quantise_w1(1, 0, 0, 2, nc.vector.tensor_copy, placed("w1_bf100", [P, 2, P, PACK], BF16, 21))
        quantise_w1(1, 0, 2, 2, nc.scalar.copy, pair_tile("w1_bf101"))
        for t in range(PACK):
            stage1_pass(1, 0, t)

        empty_h(0, 0)
        w2_codes = keep.tile([P, 4 * H], U8, name="w2_codes", align_bytes=64)
        nc.vector.tensor_copy(
            w2_codes[:].bitcast(U16).rearrange("p (g t m) -> p g t m", g=4, t=PACK),
            w2_raw[:].bitcast(U16).rearrange("p (g m t) -> p g t m", g=4, t=PACK),
        )
        pick_spawning(0, 0)
        pick_settling(0, 0)
        pair = [P, 2, P, PACK]
        wide = placed("w1_bf010", [P, 6, P, PACK], BF16, 45)
        quantise_w1(0, 1, 0, 2, gpsimd_copy, wide[:, 0:2])
        empty_h(0, 1)
        pick_spawning(0, 1, 45)
        pick_settling(0, 1, 47)
        empty_h(0, 2)
        empty_h(0, 3)
        quantise_w1(1, 1, 0, 2, nc.scalar.copy, placed("w1_bf110", pair, BF16, 53))
        pick_spawning(0, 2, 54)
        quantise_w1(0, 1, 2, 2, gpsimd_copy, placed("w1_bf012", pair, BF16, 49), 53)
        quantise_w1(1, 1, 2, 2, nc.scalar.copy, placed("w1_bf112", pair, BF16, 51))
        pick_spawning(0, 3, 50)
        for t in range(PACK):
            for a in range(2):
                stage1_pass(a, 1, t)

        x_bf = [
            placed("x_bf0", [P, PACK, E], BF16, 56),
            keep.tile([P, PACK, E], BF16, name="x_bf1", align_bytes=64),
        ]

        def activate(a, t):
            act = edge_tile("act%d%d" % (a, t), 25 + 2 * t if a == 0 else None)
            nc.scalar.activation(act[:], hp[a, t][:], ACT.Gelu_apprx_tanh, bias=zero_bias[:])
            factor = half_gain[:, a, t : t + 1]
            if (a, t) == (1, 3):
                nc.scalar.activation(x_bf[a][:, t, :], act[:], ACT.Copy, scale=factor)
            else:
                nc.gpsimd.tensor_scalar(x_bf[a][:, t, :], act[:], factor, 0.0, ALU.mult, ALU.add)

        for t0 in (0, 2):
            for t in (t0, t0 + 1):
                empty_h(1, t)
                pick_spawning(1, t)
            for t in (t0, t0 + 1):
                activate(0, t)
        for t in range(PACK):
            activate(1, t)

        x_codes = {}
        x_sc = {}

        def quantise_x(a, engine_copy):
            grouped = keep.tile([P, E, PACK], BF16, name="x_grouped%d" % a, tag=("act13", "x_grouped1")[a], align_bytes=64)
            engine_copy(
                grouped[:].rearrange("p (c i) t -> p c t i", i=4),
                x_bf[a][:].rearrange("p t (c i) -> p c t i", i=4),
            )
            x_codes[a] = keep.tile([P, E], U32, name="x_codes%d" % a, align_bytes=64)
            x_sc[a] = keep.tile([P, E], U8, name="x_sc%d" % a, align_bytes=64)
            nc.vector.quantize_mx(
                out=x_codes[a][:].bitcast(FP8X4),
                scales=x_sc[a][:],
                in_=grouped[:].rearrange("p m t -> p (m t)"),
            )

        pick_settling(0, 2, "hp10")
        pick_settling(0, 3, "hp11")
        pick_settling(1, 0, "hp12")
        quantise_x(1, nc.vector.tensor_copy)
        quantise_x(0, nc.scalar.copy)
        pick_settling(1, 1, "act13")

        tiles = [(b, t) for b in range(2) for t in range(PACK)]
        y_ps = {}
        for b, t in tiles:
            y_ps[b, t] = bank(PACK * b + t, "y_ps%d%d" % (b, t))
            for a in range(2):
                first = ((2 * a + b) * PACK + t) * P
                nc.tensor.matmul_mx(
                    out=y_ps[b, t][:],
                    lhsT=w2_codes[:, 2 * first : 2 * (first + P)].bitcast(FP4X4),
                    lhsT_scale=w2_sc[:, first : first + P],
                    rhs=x_codes[a][:].bitcast(FP8X4),
                    rhs_scale=x_sc[a][:],
                    start=(a == 0),
                    stop=(a == 1),
                )

        out_rows = out.rearrange("(b p t) m -> b t p m", b=2, t=PACK)
        gated = keep.tile([P, 2, PACK, E], F32, name="gated", align_bytes=64)
        first_th = placed("first_th", [P, 2, E], F32, 56)
        second_th = placed("second_th", [P, 2, E], F32, 60)
        later_th = keep.tile([P, 4, E], F32, name="later_th", align_bytes=64)

        def gate(i):
            b, t = tiles[i]
            if i < 2:
                th = first_th[:, i, :]
            elif i < 4:
                th = second_th[:, i - 2, :]
            else:
                th = later_th[:, i - 4, :]
            nc.scalar.activation(th, hs[b, t][:], ACT.Tanh, bias=zero_bias[:], scale=0.5)
            nc.vector.scalar_tensor_tensor(gated[:, b, t, :], th, 1.0, y_ps[b, t][:], ALU.add, ALU.mult)

        def finish(i):
            b, t = tiles[i]
            res = keep.tile([P, E], F32, name="res%d%d" % (b, t), align_bytes=64)
            halves = [slice(0, E // 2), slice(E // 2, E)]
            if i < 5:
                nc.gpsimd.tensor_tensor(res[:], gated[:, b, t, :], hs[b, t][:], ALU.add)
            elif i < 7:
                nc.vector.tensor_tensor(res[:], gated[:, b, t, :], hs[b, t][:], ALU.add)
            else:
                for cols in halves:
                    nc.vector.tensor_tensor(res[:, cols], gated[:, b, t, cols], hs[b, t][:, cols], ALU.add)
                    nc.sync.dma_start(out_rows[b, t][:, cols], res[:, cols])
                return
            nc.sync.dma_start(out_rows[b, t], res[:])

        gate(0)
        gate(1)
        pick_settling(1, 2, 56)
        gate(2)
        gate(3)
        pick_settling(1, 3, 60)
        for i in range(4, len(tiles)):
            gate(i)
        for i in range(len(tiles)):
            finish(i)
